import numpy as np
import ml_dtypes


def mxq(x, axis, fmt="e4m3"):
    dtype, down = {"e4m3": (ml_dtypes.float8_e4m3fn, 7), "e5m2": (ml_dtypes.float8_e5m2, 14)}[fmt]
    v = np.moveaxis(np.asarray(x, np.float32).astype(ml_dtypes.bfloat16).astype(np.float64), axis, -1)
    blocks = v.reshape(v.shape[:-1] + (-1, 32))
    amax = np.abs(blocks).max(-1, keepdims=True)
    byte = np.maximum(np.where(amax > 0, np.frexp(amax)[1] - 1 + 127, 0) - down, 1)
    scale = np.exp2(byte - 127.0)
    codes = (blocks / scale).astype(np.float32).astype(dtype).astype(np.float64)
    return np.moveaxis((codes * scale).reshape(v.shape), -1, axis)


WIDE = False


def mx_kscale(k):
    if not WIDE:
        return np.ones(k)
    levels = np.array([30, -30])
    if k % 512:
        return np.exp2(np.random.permutation(np.resize(levels, k // 32))).repeat(32)
    a = np.empty((k // 512, 16))
    for p in range(k // 512):
        a[p, :8] = np.random.permutation(np.resize(levels, 8))
        for g in range(8):
            far = levels[np.abs(levels - a[p, g]) >= 10]
            a[p, g + 8] = far[np.random.randint(len(far))]
    return np.exp2(a.ravel()).repeat(32)


def f64(x):
    return np.asarray(x).astype(np.float64)


def striped(idx):
    return np.tile(idx.reshape(-1, 16).T, (8, 1)).astype(np.uint16)


def unstriped(offs):
    return offs[:16].T.reshape(-1).astype(np.int64)


def d_relu(v):
    return (v > 0).astype(np.float64)


K, T, E, C, H, N = 256, 1536, 2, 512, 512, 512


def by_expert(wq, xq):
    return np.concatenate([wq[e].T @ xq[:, e * C:(e + 1) * C] for e in range(E)], axis=1)


def setup_inputs():
    n = np.random.standard_normal
    slot_token = np.random.permutation(T)[:E * C]
    s = mx_kscale(N)[:, None]
    z = np.ones(T); z[slot_token] = mx_kscale(E * C)
    return {
        "xT": (n((K, T)) * z[None, :]).astype(np.float32),
        "dyT": (n((N, T)) * s).astype(np.float32),
        "a": n((H, E * C)).astype(np.float32),
        "w2": (n((E, N, H)) / np.sqrt(N) / s[None]).astype(np.float32),
        "gate": np.tile(np.random.uniform(0.2, 1.0, E * C) / z[slot_token], (N, 1)).astype(np.float32),
        "offs": striped(slot_token),
    }


def reference(xT, dyT, a, w2, gate, offs):
    idx = unstriped(offs)
    gq = mxq(f64(gate) * f64(dyT)[:, idx], 0, "e5m2")
    dh = by_expert(mxq(f64(w2), 1, "e4m3"), gq)
    da = mxq(dh * d_relu(f64(a)), 1, "e5m2")
    xq = mxq(f64(xT)[:, idx], 1, "e4m3")
    return np.stack([(xq[:, e * C:(e + 1) * C] @ da[:, e * C:(e + 1) * C].T) for e in range(E)])

@@ -1,0 +1,261 @@
+from contextlib import ExitStack
+
+import concourse.mybir as mybir
+from concourse.masks import make_identity
+
+K, T, E, C, H, N = 256, 1536, 2, 512, 512, 512
+FLOPS = 2 * E * C * H * (N + K)
+
+F32 = mybir.dt.float32
+BF16 = mybir.dt.bfloat16
+U32 = mybir.dt.uint32
+U16 = mybir.dt.uint16
+U8 = mybir.dt.uint8
+E4M3 = mybir.dt.float8_e4m3fn_x4
+E5M2 = mybir.dt.float8_e5m2_x4
+COPY = mybir.ActivationFunctionType.Copy
+IS_GT = mybir.AluOpType.is_gt
+MULT = mybir.AluOpType.mult
+ADD = mybir.AluOpType.add
+
+P = 128
+PACK = 4
+BLOCKS = C // P
+LIST_COLS = C // 16
+
+
+def tile_moe_mlp_relu_kernel(tc, xT, dyT, a, w2, gate, offs, out):
+    nc = tc.nc
+    with ExitStack() as ctx:
+        keep = ctx.enter_context(tc.tile_pool(name="keep", bufs=1))
+        turn_in = ctx.enter_context(tc.psum_pool(name="turn_in", bufs=2))
+        turn_words = ctx.enter_context(tc.psum_pool(name="turn_words", bufs=2))
+        sums = ctx.enter_context(tc.psum_pool(name="sums", bufs=4))
+
+        shared = {"g_codes0":"w_raw1_1","x_picked0_1":"g_in0","x_picked1_1":"w_in1","g_codes1":"a_raw0_0"}
+
+        def sb(name, shape, dtype):
+            return keep.tile(shape, dtype, name=name, tag=shared.get(name, name), align_bytes=64)
+
+        offsets = keep.tile([P, E * LIST_COLS], U16, name="offsets")
+        identity = sb("identity", [P, P], F32)
+        gate_rows = sb("gate_rows", [P, P], F32)
+        gate_cols = sb("gate_cols", [P, E * BLOCKS], F32)
+        dy = [sb("dy%d" % t, [P, T], F32) for t in range(PACK)]
+        x_raw = [sb("x_raw%d" % b, [P, T], F32) for b in range(K // P)]
+        w_raw = [[sb("w_raw%d_%d" % (e, h), [P, PACK, H // 2], F32) for h in range(2)] for e in range(E)]
+        a_raw = [[sb("a_raw%d_%d" % (e, b), [P, C], F32) for b in range(H // P)] for e in range(E)]
+
+        nc.vector.memset(gate_rows[:], 0.0)
+        make_identity(nc, identity[:])
+
+        dy_rows = dyT.rearrange("(p t) c -> p t c", t=PACK)
+
+        def load_dy(t):
+            nc.sync.dma_start(out=dy[t][:], in_=dy_rows[:, t, :])
+
+        def load_x(b):
+            nc.sync.dma_start(out=x_raw[b][:], in_=xT[b * P:(b + 1) * P, :])
+
+        def load_w(e):
+            for h in range(2):
+                rows = w2[e].rearrange("(p t) i -> p t i", t=PACK)
+                nc.sync.dma_start(out=w_raw[e][h][:], in_=rows[:, :, h * H // 2:(h + 1) * H // 2])
+
+        def load_a(e):
+            for b in range(H // P):
+                nc.sync.dma_start(out=a_raw[e][b][:], in_=a[b * P:(b + 1) * P, e * C:(e + 1) * C])
+
+        load_dy(0)
+        nc.sync.dma_start(offsets[:], offs)
+        nc.scalar.dma_start(out=gate_rows[0:E * BLOCKS, :], in_=gate[0, :].rearrange("(c j) -> c j", j=P))
+        load_dy(1)
+        load_x(0)
+        load_dy(2)
+        load_dy(3)
+        load_x(1)
+        load_w(0)
+        load_w(1)
+        load_a(0)
+        load_a(1)
+
+        gate_bank = turn_words.tile([P, 4, P], F32, name="gate_bank", tag="words")
+        nc.tensor.transpose(gate_bank[:, 0, :], gate_rows[:], identity[:])
+        nc.scalar.copy(gate_cols[:], gate_bank[:, 0, 0:E * BLOCKS])
+
+        def slots(e):
+            return offsets[:, e * LIST_COLS:(e + 1) * LIST_COLS]
+
+        picked = [[sb("picked%d_%d" % (e, t), [P, C], F32) for t in range(PACK)] for e in range(E)]
+        g_rows = [[sb("g_rows%d_%d" % (e, s), [P, 2, P, 2], BF16) for s in range(BLOCKS)] for e in range(E)]
+        g_in = [sb("g_in%d" % e, [P, C * PACK], BF16) for e in range(E)]
+        g_codes = {}
+        g_scales = [sb("g_scales%d" % e, [P, C], U8) for e in range(E)]
+        w_in = [sb("w_in%d" % e, [P, H, PACK], BF16) for e in range(E)]
+        w_codes = [sb("w_codes%d" % e, [P, H], U32) for e in range(E)]
+        w_scales = [sb("w_scales%d" % e, [P, H], U8) for e in range(E)]
+        x_cast = [sb("x_cast%d" % b, [P, T], BF16) for b in range(K // P)]
+        x_picked = [{} for e in range(E)]
+        x_in = [sb("x_in%d" % e, [P, K * PACK], BF16) for e in range(E)]
+        x_codes = [sb("x_codes%d" % e, [P, K], U32) for e in range(E)]
+        x_scales = [sb("x_scales%d" % e, [P, K], U8) for e in range(E)]
+        da_rows = [[sb("da_rows%d_%d" % (e, b), [P, C], BF16) for b in range(H // P)] for e in range(E)]
+        da_in = [[sb("da_in%d_%d" % (e, h), [P, H * PACK // 2], BF16) for h in range(2)] for e in range(E)]
+        da_codes = [sb("da_codes%d" % e, [P, H], U32) for e in range(E)]
+        da_scales = [sb("da_scales%d" % e, [P, H], U8) for e in range(E)]
+        result = [[sb("result%d_%d" % (e, b), [P, H], F32) for b in range(K // P)] for e in range(E)]
+
+        def gather_dy(e, t):
+            nc.vector.tensor_copy(picked[e][t][:], dy[t][:].indirect(slots(e)))
+
+        def gate_half(e, u):
+            for pair in range(BLOCKS // 2):
+                bank = turn_in.tile([P, 2, 2, P], F32, name="bank_in")
+                for s in range(2):
+                    for r in range(2):
+                        cols = slice((2 * pair + s) * P, (2 * pair + s + 1) * P)
+                        nc.tensor.transpose(bank[:, s, r, :], picked[e][2 * u + r][:, cols], identity[:])
+                for s in range(2):
+                    block = 2 * pair + s
+                    column = e * BLOCKS + block
+                    nc.scalar.activation(
+                        g_rows[e][block][:, u, :, :],
+                        bank[:, s, :, :].rearrange("j r p -> j p r"),
+                        COPY,
+                        scale=gate_cols[:, column:column + 1],
+                    )
+
+        def turn_pairs(pool, sources, step, target, engine):
+            count = len(sources)
+            bank = pool.tile([P, 2, 2, P], F32, name="bank_words", tag="words")
+            for s in range(count):
+                for u in range(2):
+                    picked_words = sources[s][:, u::2] if step == 2 else sources[s][:, u * P:(u + 1) * P]
+                    nc.tensor.transpose(bank[:, s, u, :], picked_words, identity[:])
+            engine(
+                target.rearrange("p (s c u) -> p s c u", s=count, u=2),
+                bank[:, 0:count, :, :].rearrange("p s u c -> p s c u"),
+            )
+
+        def turn_g(e):
+            words = g_in[e][:].bitcast(F32)
+            for pair in range(BLOCKS // 2):
+                sources = [g_rows[e][2 * pair + s][:].rearrange("j u p r -> j (u p r)").bitcast(F32) for s in range(2)]
+                turn_pairs(turn_words, sources, 1, words[:, pair * 4 * P:(pair + 1) * 4 * P], nc.scalar.copy)
+
+        def quantize(codes, scales, values, fmt):
+            nc.vector.quantize_mx(out=codes[:].bitcast(fmt), scales=scales[:], in_=values)
+
+        def quantize_g(e):
+            g_codes[e] = sb("g_codes%d" % e, [P, C], U32)
+            quantize(g_codes[e], g_scales[e], g_in[e][:], E5M2)
+
+        def quantize_w(e):
+            quantize(w_codes[e], w_scales[e], flat(w_in[e]), E4M3)
+
+        def quantize_x(e):
+            quantize(x_codes[e], x_scales[e], x_in[e][:], E4M3)
+
+        def weave_w(e, h):
+            nc.vector.tensor_copy(
+                w_in[e][:, h * H // 2:(h + 1) * H // 2, :].rearrange("p (c i) t -> p c t i", i=4),
+                w_raw[e][h][:].rearrange("p t (c i) -> p c t i", i=4),
+            )
+
+        def cast_x(b):
+            nc.gpsimd.tensor_scalar(x_cast[b][:], x_raw[b][:], 1.0, 0.0, MULT, ADD)
+
+        def gather_x(e, b):
+            x_picked[e][b] = sb("x_picked%d_%d" % (e, b), [P, C], BF16)
+            nc.scalar.activation(x_picked[e][b][:], x_cast[b][:].indirect(slots(e)), COPY)
+
+        def turn_x(e):
+            turn_pairs(sums, [x_picked[e][b][:].bitcast(F32) for b in range(2)], 2, x_in[e][:].bitcast(F32), nc.scalar.copy)
+
+        def first_product(e, b):
+            cols = slice(b * P, (b + 1) * P)
+            dh = sums.tile([P, C], F32, name="dh", tag="words")
+            nc.tensor.matmul_mx(
+                out=dh[:], lhsT=w_codes[e][:, cols].bitcast(E4M3), lhsT_scale=w_scales[e][:, cols],
+                rhs=g_codes[e][:].bitcast(E5M2), rhs_scale=g_scales[e][:], start=True, stop=True,
+            )
+            nc.vector.scalar_tensor_tensor(da_rows[e][b][:], a_raw[e][b][:], 0.0, dh[:], IS_GT, MULT)
+
+        def turn_da(e, first, count, engine):
+            words = da_in[e][first // 2][:].bitcast(F32)
+            sources = [da_rows[e][first + s][:].bitcast(F32) for s in range(count)]
+            start = (first % 2) * 2 * P
+            turn_pairs(turn_words, sources, 2, words[:, start:start + count * 2 * P], engine)
+
+        def quantize_da(e, half):
+            cols = slice(half * 2 * P, (half + 1) * 2 * P)
+            nc.vector.quantize_mx(out=da_codes[e][:, cols].bitcast(E5M2), scales=da_scales[e][:, cols], in_=da_in[e][half][:])
+
+        def second_product(e):
+            for b in range(K // P):
+                cols = slice(b * P, (b + 1) * P)
+                dw = sums.tile([P, H], F32, name="dw", tag="words")
+                nc.tensor.matmul_mx(
+                    out=dw[:], lhsT=x_codes[e][:, cols].bitcast(E4M3), lhsT_scale=x_scales[e][:, cols],
+                    rhs=da_codes[e][:].bitcast(E5M2), rhs_scale=da_scales[e][:], start=True, stop=True,
+                )
+                if e == E - 1 and b == 1:
+                    nc.vector.tensor_copy(result[e][b][:], dw[:])
+                else:
+                    nc.scalar.copy(result[e][b][:], dw[:])
+                nc.sync.dma_start(out=out[e, cols, :], in_=result[e][b][:])
+
+        def flat(tile3):
+            return tile3[:].rearrange("p i t -> p (i t)")
+
+        gather_dy(0, 0)
+        gather_dy(1, 0)
+        gather_dy(0, 1)
+        gather_dy(1, 1)
+        cast_x(0)
+        gate_half(0, 0)
+        gate_half(1, 0)
+        gather_dy(0, 2)
+        gather_dy(1, 2)
+        gather_dy(0, 3)
+        gather_dy(1, 3)
+        cast_x(1)
+        gather_x(0, 0)
+        gather_x(1, 0)
+        gate_half(0, 1)
+        turn_g(0)
+        gate_half(1, 1)
+        turn_g(1)
+        weave_w(0, 0)
+        weave_w(0, 1)
+        quantize_w(0)
+        weave_w(1, 0)
+        weave_w(1, 1)
+        quantize_g(0)
+        quantize_w(1)
+        first_product(0, 0)
+        quantize_g(1)
+        first_product(0, 1)
+        first_product(0, 2)
+        first_product(0, 3)
+        gather_x(0, 1)
+        gather_x(1, 1)
+        first_product(1, 0)
+        first_product(1, 1)
+        turn_da(0, 0, 2, nc.scalar.copy)
+        first_product(1, 2)
+        first_product(1, 3)
+        turn_da(0, 2, 2, nc.scalar.copy)
+        turn_x(0)
+        turn_da(1, 0, 2, nc.scalar.copy)
+        turn_x(1)
+        turn_da(1, 2, 1, nc.scalar.copy)
+        turn_da(1, 3, 1, nc.scalar.copy)
+        quantize_da(0, 0)
+        quantize_da(0, 1)
+        quantize_x(0)
+        quantize_da(1, 0)
+        quantize_x(1)
+        quantize_da(1, 1)
+        second_product(0)
+        second_product(1)

@@ -20,7 +20,6 @@ ADD = mybir.AluOpType.add
 
 P = 128
 PACK = 4
-BLOCKS = C // P
 LIST_COLS = C // 16
 
 
@@ -28,234 +27,253 @@ def tile_moe_mlp_relu_kernel(tc, xT, dyT, a, w2, gate, offs, out):
     nc = tc.nc
     with ExitStack() as ctx:
         keep = ctx.enter_context(tc.tile_pool(name="keep", bufs=1))
-        turn_in = ctx.enter_context(tc.psum_pool(name="turn_in", bufs=2))
-        turn_words = ctx.enter_context(tc.psum_pool(name="turn_words", bufs=2))
+        turns = ctx.enter_context(tc.psum_pool(name="turns", bufs=4))
         sums = ctx.enter_context(tc.psum_pool(name="sums", bufs=4))
 
-        shared = {"g_codes0":"w_raw1_1","x_picked0_1":"g_in0","x_picked1_1":"w_in1","g_codes1":"a_raw0_0"}
+        shared = {}
+        tiles = {}
 
         def sb(name, shape, dtype):
-            return keep.tile(shape, dtype, name=name, tag=shared.get(name, name), align_bytes=64)
+            if name not in tiles:
+                tiles[name] = keep.tile(shape, dtype, name=name, tag=shared.get(name, name), align_bytes=64)
+            return tiles[name]
 
         offsets = keep.tile([P, E * LIST_COLS], U16, name="offsets")
         identity = sb("identity", [P, P], F32)
-        gate_rows = sb("gate_rows", [P, P], F32)
-        gate_cols = sb("gate_cols", [P, E * BLOCKS], F32)
-        dy = [sb("dy%d" % t, [P, T], F32) for t in range(PACK)]
-        x_raw = [sb("x_raw%d" % b, [P, T], F32) for b in range(K // P)]
-        w_raw = [[sb("w_raw%d_%d" % (e, h), [P, PACK, H // 2], F32) for h in range(2)] for e in range(E)]
-        a_raw = [[sb("a_raw%d_%d" % (e, b), [P, C], F32) for b in range(H // P)] for e in range(E)]
-
-        nc.vector.memset(gate_rows[:], 0.0)
         make_identity(nc, identity[:])
 
-        dy_rows = dyT.rearrange("(p t) c -> p t c", t=PACK)
+        def dy(t):
+            return sb("dy%d" % t, [P, T], F32)
+
+        def gates(e):
+            return sb("gates%d" % e, [P, C], F32)
+
+        def x_raw(b):
+            return sb("x_raw%d" % b, [P, T], F32)
+
+        def w_raw(e):
+            return sb("w_raw%d" % e, [P, PACK, H], F32)
+
+        def a_raw(e, b):
+            return sb("a_raw%d_%d" % (e, b), [P, C], F32)
+
+        def g_rows(e):
+            return sb("g_rows%d" % e, [P, PACK, C], F32)
+
+        def g_in(e):
+            return sb("g_in%d" % e, [P, C, PACK], BF16)
+
+        def w_in(e):
+            return sb("w_in%d" % e, [P, H, PACK], BF16)
+
+        def x_cast(b):
+            return sb("x_cast%d" % b, [P, T], BF16)
+
+        def x_picked(e, b):
+            return sb("x_picked%d_%d" % (e, b), [P, C], BF16)
+
+        def x_in(e):
+            return sb("x_in%d" % e, [P, K * PACK], BF16)
+
+        def da_rows(e, b):
+            return sb("da_rows%d_%d" % (e, b), [P, C], BF16)
+
+        def da_in(e, h):
+            return sb("da_in%d_%d" % (e, h), [P, H * PACK // 2], BF16)
+
+        def codes(name, e, width):
+            return sb("%s_codes%d" % (name, e), [P, width], U32)
+
+        def scales(name, e, width):
+            return sb("%s_scales%d" % (name, e), [P, width], U8)
 
         def load_dy(t):
-            nc.sync.dma_start(out=dy[t][:], in_=dy_rows[:, t, :])
+            nc.sync.dma_start(out=dy(t)[:], in_=dyT.rearrange("(p t) c -> p t c", t=PACK)[:, t, :])
+
+        def load_gate(e):
+            nc.sync.dma_start(out=gates(e)[:], in_=gate[0:P, e * C:(e + 1) * C])
 
         def load_x(b):
-            nc.sync.dma_start(out=x_raw[b][:], in_=xT[b * P:(b + 1) * P, :])
+            nc.sync.dma_start(out=x_raw(b)[:], in_=xT[b * P:(b + 1) * P, :])
 
         def load_w(e):
-            for h in range(2):
-                rows = w2[e].rearrange("(p t) i -> p t i", t=PACK)
-                nc.sync.dma_start(out=w_raw[e][h][:], in_=rows[:, :, h * H // 2:(h + 1) * H // 2])
+            nc.sync.dma_start(out=w_raw(e)[:], in_=w2[e].rearrange("(p t) i -> p t i", t=PACK))
 
         def load_a(e):
             for b in range(H // P):
-                nc.sync.dma_start(out=a_raw[e][b][:], in_=a[b * P:(b + 1) * P, e * C:(e + 1) * C])
-
-        load_dy(0)
-        nc.sync.dma_start(offsets[:], offs)
-        nc.scalar.dma_start(out=gate_rows[0:E * BLOCKS, :], in_=gate[0, :].rearrange("(c j) -> c j", j=P))
-        load_dy(1)
-        load_x(0)
-        load_dy(2)
-        load_dy(3)
-        load_x(1)
-        load_w(0)
-        load_w(1)
-        load_a(0)
-        load_a(1)
-
-        gate_bank = turn_words.tile([P, 4, P], F32, name="gate_bank", tag="words")
-        nc.tensor.transpose(gate_bank[:, 0, :], gate_rows[:], identity[:])
-        nc.scalar.copy(gate_cols[:], gate_bank[:, 0, 0:E * BLOCKS])
+                nc.sync.dma_start(out=a_raw(e, b)[:], in_=a[b * P:(b + 1) * P, e * C:(e + 1) * C])
 
         def slots(e):
             return offsets[:, e * LIST_COLS:(e + 1) * LIST_COLS]
 
-        picked = [[sb("picked%d_%d" % (e, t), [P, C], F32) for t in range(PACK)] for e in range(E)]
-        g_rows = [[sb("g_rows%d_%d" % (e, s), [P, 2, P, 2], BF16) for s in range(BLOCKS)] for e in range(E)]
-        g_in = [sb("g_in%d" % e, [P, C * PACK], BF16) for e in range(E)]
-        g_codes = {}
-        g_scales = [sb("g_scales%d" % e, [P, C], U8) for e in range(E)]
-        w_in = [sb("w_in%d" % e, [P, H, PACK], BF16) for e in range(E)]
-        w_codes = [sb("w_codes%d" % e, [P, H], U32) for e in range(E)]
-        w_scales = [sb("w_scales%d" % e, [P, H], U8) for e in range(E)]
-        x_cast = [sb("x_cast%d" % b, [P, T], BF16) for b in range(K // P)]
-        x_picked = [{} for e in range(E)]
-        x_in = [sb("x_in%d" % e, [P, K * PACK], BF16) for e in range(E)]
-        x_codes = [sb("x_codes%d" % e, [P, K], U32) for e in range(E)]
-        x_scales = [sb("x_scales%d" % e, [P, K], U8) for e in range(E)]
-        da_rows = [[sb("da_rows%d_%d" % (e, b), [P, C], BF16) for b in range(H // P)] for e in range(E)]
-        da_in = [[sb("da_in%d_%d" % (e, h), [P, H * PACK // 2], BF16) for h in range(2)] for e in range(E)]
-        da_codes = [sb("da_codes%d" % e, [P, H], U32) for e in range(E)]
-        da_scales = [sb("da_scales%d" % e, [P, H], U8) for e in range(E)]
-        result = [[sb("result%d_%d" % (e, b), [P, H], F32) for b in range(K // P)] for e in range(E)]
-
         def gather_dy(e, t):
-            nc.vector.tensor_copy(picked[e][t][:], dy[t][:].indirect(slots(e)))
+            nc.vector.tensor_tensor(g_rows(e)[:, t, :], dy(t)[:].indirect(slots(e)), gates(e)[:], MULT)
 
-        def gate_half(e, u):
-            for pair in range(BLOCKS // 2):
-                bank = turn_in.tile([P, 2, 2, P], F32, name="bank_in")
-                for s in range(2):
-                    for r in range(2):
-                        cols = slice((2 * pair + s) * P, (2 * pair + s + 1) * P)
-                        nc.tensor.transpose(bank[:, s, r, :], picked[e][2 * u + r][:, cols], identity[:])
-                for s in range(2):
-                    block = 2 * pair + s
-                    column = e * BLOCKS + block
-                    nc.scalar.activation(
-                        g_rows[e][block][:, u, :, :],
-                        bank[:, s, :, :].rearrange("j r p -> j p r"),
-                        COPY,
-                        scale=gate_cols[:, column:column + 1],
-                    )
+        def weave(copy, woven, rows, first, last):
+            copy(
+                woven[:, first:last, :].rearrange("p (c i) t -> p c t i", i=4),
+                rows[:, :, first:last].rearrange("p t (c i) -> p c t i", i=4),
+            )
 
-        def turn_pairs(pool, sources, step, target, engine):
-            count = len(sources)
-            bank = pool.tile([P, 2, 2, P], F32, name="bank_words", tag="words")
+        def gate_weave(e, first, last):
+            nc.vector.tensor_tensor(
+                g_in(e)[:, first:last, :].rearrange("p (c i) t -> p c t i", i=4),
+                g_rows(e)[:, :, first:last].rearrange("p t (c i) -> p c t i", i=4),
+                gates(e)[:, first:last].rearrange("p (c i) -> p c i", i=4).unsqueeze(2).to_broadcast([P, (last - first) // 4, PACK, 4]),
+                MULT,
+            )
+
+        def pool_copy(target, source):
+            nc.gpsimd.tensor_scalar(target, source, 1.0, 0.0, MULT, ADD)
+
+        def weave_g(e, first=0, last=C, copy=nc.scalar.copy):
+            weave(copy, g_in(e), g_rows(e), first, last)
+
+        def weave_w(e, first=0, last=H, copy=nc.vector.tensor_copy):
+            weave(copy, w_in(e), w_raw(e), first, last)
+
+        def quantize(name, e, width, values, fmt, cols):
+            nc.vector.quantize_mx(out=codes(name, e, width)[:, cols].bitcast(fmt), scales=scales(name, e, width)[:, cols], in_=values)
+
+        def quantize_g(e):
+            quantize("g", e, C, g_in(e)[:].rearrange("p c t -> p (c t)"), E5M2, slice(0, C))
+
+        def quantize_w(e):
+            quantize("w", e, H, w_in(e)[:].rearrange("p c t -> p (c t)"), E4M3, slice(0, H))
+
+        def quantize_x(e):
+            quantize("x", e, K, x_in(e)[:], E4M3, slice(0, K))
+
+        def quantize_da(e, h):
+            quantize("da", e, H, da_in(e, h)[:], E5M2, slice(h * H // 2, (h + 1) * H // 2))
+
+        def cast_x(b, copy=nc.scalar.copy):
+            copy(x_cast(b)[:], x_raw(b)[:])
+
+        def gather_x(e, b):
+            nc.scalar.activation(x_picked(e, b)[:], x_cast(b)[:].indirect(slots(e)), COPY)
+
+        def turn(pool, halves, target, copy):
+            count = len(halves)
+            bank = pool.tile([P, 2, 2, P], F32, name="bank", tag="bank")
             for s in range(count):
                 for u in range(2):
-                    picked_words = sources[s][:, u::2] if step == 2 else sources[s][:, u * P:(u + 1) * P]
-                    nc.tensor.transpose(bank[:, s, u, :], picked_words, identity[:])
-            engine(
+                    nc.tensor.transpose(bank[:, s, u, :], halves[s][u], identity[:])
+            copy(
                 target.rearrange("p (s c u) -> p s c u", s=count, u=2),
                 bank[:, 0:count, :, :].rearrange("p s u c -> p s c u"),
             )
 
-        def turn_g(e):
-            words = g_in[e][:].bitcast(F32)
-            for pair in range(BLOCKS // 2):
-                sources = [g_rows[e][2 * pair + s][:].rearrange("j u p r -> j (u p r)").bitcast(F32) for s in range(2)]
-                turn_pairs(turn_words, sources, 1, words[:, pair * 4 * P:(pair + 1) * 4 * P], nc.scalar.copy)
+        def turn_x(e, first=0, count=2, pool=turns, copy=nc.scalar.copy):
+            words = [x_picked(e, first + b)[:].bitcast(F32) for b in range(count)]
+            target = x_in(e)[:].bitcast(F32)[:, first * 2 * P:(first + count) * 2 * P]
+            turn(pool, [[w[:, u::2] for u in range(2)] for w in words], target, copy)
 
-        def quantize(codes, scales, values, fmt):
-            nc.vector.quantize_mx(out=codes[:].bitcast(fmt), scales=scales[:], in_=values)
+        def turn_da(e, first, count, pool=turns, copy=nc.scalar.copy):
+            words = [da_rows(e, first + s)[:].bitcast(F32) for s in range(count)]
+            start = (first % 2) * 2 * P
+            target = da_in(e, first // 2)[:].bitcast(F32)[:, start:start + count * 2 * P]
+            turn(pool, [[w[:, u * P:(u + 1) * P] for u in range(2)] for w in words], target, copy)
 
-        def quantize_g(e):
-            g_codes[e] = sb("g_codes%d" % e, [P, C], U32)
-            quantize(g_codes[e], g_scales[e], g_in[e][:], E5M2)
-
-        def quantize_w(e):
-            quantize(w_codes[e], w_scales[e], flat(w_in[e]), E4M3)
-
-        def quantize_x(e):
-            quantize(x_codes[e], x_scales[e], x_in[e][:], E4M3)
-
-        def weave_w(e, h):
-            nc.vector.tensor_copy(
-                w_in[e][:, h * H // 2:(h + 1) * H // 2, :].rearrange("p (c i) t -> p c t i", i=4),
-                w_raw[e][h][:].rearrange("p t (c i) -> p c t i", i=4),
+        def product(left, right, e, b, width, bank):
+            cols = slice(b * P, (b + 1) * P)
+            nc.tensor.matmul_mx(
+                out=bank[:],
+                lhsT=codes(left, e, width)[:, cols].bitcast(E4M3), lhsT_scale=scales(left, e, width)[:, cols],
+                rhs=codes(right, e, C)[:].bitcast(E5M2), rhs_scale=scales(right, e, C)[:],
+                start=True, stop=True,
             )
 
-        def cast_x(b):
-            nc.gpsimd.tensor_scalar(x_cast[b][:], x_raw[b][:], 1.0, 0.0, MULT, ADD)
-
-        def gather_x(e, b):
-            x_picked[e][b] = sb("x_picked%d_%d" % (e, b), [P, C], BF16)
-            nc.scalar.activation(x_picked[e][b][:], x_cast[b][:].indirect(slots(e)), COPY)
-
-        def turn_x(e):
-            turn_pairs(sums, [x_picked[e][b][:].bitcast(F32) for b in range(2)], 2, x_in[e][:].bitcast(F32), nc.scalar.copy)
+        banks = {}
 
         def first_product(e, b):
-            cols = slice(b * P, (b + 1) * P)
-            dh = sums.tile([P, C], F32, name="dh", tag="words")
-            nc.tensor.matmul_mx(
-                out=dh[:], lhsT=w_codes[e][:, cols].bitcast(E4M3), lhsT_scale=w_scales[e][:, cols],
-                rhs=g_codes[e][:].bitcast(E5M2), rhs_scale=g_scales[e][:], start=True, stop=True,
-            )
-            nc.vector.scalar_tensor_tensor(da_rows[e][b][:], a_raw[e][b][:], 0.0, dh[:], IS_GT, MULT)
+            banks[e, b] = sums.tile([P, C], F32, name="dh", tag="bank")
+            product("w", "g", e, b, H, banks[e, b])
 
-        def turn_da(e, first, count, engine):
-            words = da_in[e][first // 2][:].bitcast(F32)
-            sources = [da_rows[e][first + s][:].bitcast(F32) for s in range(count)]
-            start = (first % 2) * 2 * P
-            turn_pairs(turn_words, sources, 2, words[:, start:start + count * 2 * P], engine)
-
-        def quantize_da(e, half):
-            cols = slice(half * 2 * P, (half + 1) * 2 * P)
-            nc.vector.quantize_mx(out=da_codes[e][:, cols].bitcast(E5M2), scales=da_scales[e][:, cols], in_=da_in[e][half][:])
-
-        def second_product(e):
-            for b in range(K // P):
-                cols = slice(b * P, (b + 1) * P)
-                dw = sums.tile([P, H], F32, name="dw", tag="words")
-                nc.tensor.matmul_mx(
-                    out=dw[:], lhsT=x_codes[e][:, cols].bitcast(E4M3), lhsT_scale=x_scales[e][:, cols],
-                    rhs=da_codes[e][:].bitcast(E5M2), rhs_scale=da_scales[e][:], start=True, stop=True,
+        def mask(e, b):
+            dh = banks[e, b]
+            for u in range(2):
+                nc.vector.scalar_tensor_tensor(
+                    da_rows(e, b)[:].rearrange("i (u q r) -> i u q r", u=2, r=2)[:, u],
+                    a_raw(e, b)[:].rearrange("i (q u r) -> i u q r", u=2, r=2)[:, u],
+                    0.0,
+                    dh[:].rearrange("i (q u r) -> i u q r", u=2, r=2)[:, u],
+                    IS_GT, MULT,
                 )
-                if e == E - 1 and b == 1:
-                    nc.vector.tensor_copy(result[e][b][:], dw[:])
-                else:
-                    nc.scalar.copy(result[e][b][:], dw[:])
-                nc.sync.dma_start(out=out[e, cols, :], in_=result[e][b][:])
 
-        def flat(tile3):
-            return tile3[:].rearrange("p i t -> p (i t)")
+        def second_product(e, b, copy=nc.scalar.copy):
+            dw = sums.tile([P, H], F32, name="dw", tag="bank")
+            product("x", "da", e, b, K, dw)
+            result = sb("result%d_%d" % (e, b), [P, H], F32)
+            copy(result[:], dw[:])
+            nc.sync.dma_start(out=out[e, b * P:(b + 1) * P, :], in_=result[:])
+
+        load_gate(0)
+        load_dy(0)
+        nc.sync.dma_start(offsets[:], offs)
+        load_gate(1)
+        load_dy(1)
+        load_x(0)
+        load_dy(2)
+        load_dy(3)
+        load_w(0)
+        load_w(1)
+        load_x(1)
+        load_a(0)
+        load_a(1)
 
         gather_dy(0, 0)
         gather_dy(1, 0)
         gather_dy(0, 1)
         gather_dy(1, 1)
         cast_x(0)
-        gate_half(0, 0)
-        gate_half(1, 0)
+        gather_x(0, 0)
+        gather_x(1, 0)
         gather_dy(0, 2)
         gather_dy(1, 2)
         gather_dy(0, 3)
         gather_dy(1, 3)
-        cast_x(1)
-        gather_x(0, 0)
-        gather_x(1, 0)
-        gate_half(0, 1)
-        turn_g(0)
-        gate_half(1, 1)
-        turn_g(1)
-        weave_w(0, 0)
-        weave_w(0, 1)
+        weave_g(0)
+        weave_g(1)
+        weave_w(0)
         quantize_w(0)
-        weave_w(1, 0)
-        weave_w(1, 1)
         quantize_g(0)
+        weave_w(1)
         quantize_w(1)
-        first_product(0, 0)
         quantize_g(1)
+        cast_x(1)
+        gather_x(0, 1)
+        gather_x(1, 1)
+        first_product(0, 0)
         first_product(0, 1)
         first_product(0, 2)
         first_product(0, 3)
-        gather_x(0, 1)
-        gather_x(1, 1)
+        mask(0, 0)
         first_product(1, 0)
+        mask(0, 1)
         first_product(1, 1)
-        turn_da(0, 0, 2, nc.scalar.copy)
+        mask(0, 2)
         first_product(1, 2)
+        mask(0, 3)
         first_product(1, 3)
-        turn_da(0, 2, 2, nc.scalar.copy)
+        mask(1, 0)
+        mask(1, 1)
+        mask(1, 2)
+        mask(1, 3)
+        turn_da(0, 0, 2)
+        turn_da(0, 2, 2)
         turn_x(0)
-        turn_da(1, 0, 2, nc.scalar.copy)
         turn_x(1)
-        turn_da(1, 2, 1, nc.scalar.copy)
-        turn_da(1, 3, 1, nc.scalar.copy)
+        turn_da(1, 0, 2)
+        turn_da(1, 2, 1)
+        turn_da(1, 3, 1, copy=nc.vector.tensor_copy)
         quantize_da(0, 0)
         quantize_da(0, 1)
         quantize_x(0)
         quantize_da(1, 0)
         quantize_x(1)
         quantize_da(1, 1)
-        second_product(0)
-        second_product(1)
+        second_product(0, 0)
+        second_product(0, 1)
+        second_product(1, 0)
+        second_product(1, 1, nc.vector.tensor_copy)

@@ -30,7 +30,7 @@ def tile_moe_mlp_relu_kernel(tc, xT, dyT, a, w2, gate, offs, out):
         turns = ctx.enter_context(tc.psum_pool(name="turns", bufs=4))
         sums = ctx.enter_context(tc.psum_pool(name="sums", bufs=4))
 
-        shared = {}
+        shared = {"x_cast0":"gate_cols"}
         tiles = {}
 
         def sb(name, shape, dtype):
@@ -90,8 +90,17 @@ def tile_moe_mlp_relu_kernel(tc, xT, dyT, a, w2, gate, offs, out):
         def load_dy(t):
             nc.sync.dma_start(out=dy(t)[:], in_=dyT.rearrange("(p t) c -> p t c", t=PACK)[:, t, :])
 
-        def load_gate(e):
-            nc.sync.dma_start(out=gates(e)[:], in_=gate[0:P, e * C:(e + 1) * C])
+        def gate_cols():
+            return sb("gate_cols", [P, E, PACK], F32)
+
+        def load_gate():
+            nc.sync.dma_start(out=gate_cols()[:], in_=gate[0, :].rearrange("(e q r) -> q e r", e=E, r=PACK))
+
+        def spread_gate(e):
+            bank = turns.tile([P, PACK, P], F32, name="bank", tag="bank")
+            for r in range(PACK):
+                nc.tensor.transpose(bank[:, r, :], gate_cols()[:, e, r:r + 1].to_broadcast([P, P]), identity[:])
+            nc.scalar.copy(gates(e)[:].rearrange("p (q r) -> p q r", r=PACK), bank[:].rearrange("p r q -> p q r"))
 
         def load_x(b):
             nc.sync.dma_start(out=x_raw(b)[:], in_=xT[b * P:(b + 1) * P, :])
@@ -138,8 +147,8 @@ def tile_moe_mlp_relu_kernel(tc, xT, dyT, a, w2, gate, offs, out):
         def quantize_g(e):
             quantize("g", e, C, g_in(e)[:].rearrange("p c t -> p (c t)"), E5M2, slice(0, C))
 
-        def quantize_w(e):
-            quantize("w", e, H, w_in(e)[:].rearrange("p c t -> p (c t)"), E4M3, slice(0, H))
+        def quantize_w(e, first=0, last=H):
+            quantize("w", e, H, w_in(e)[:, first:last, :].rearrange("p c t -> p (c t)"), E4M3, slice(first, last))
 
         def quantize_x(e):
             quantize("x", e, K, x_in(e)[:], E4M3, slice(0, K))
@@ -208,10 +217,9 @@ def tile_moe_mlp_relu_kernel(tc, xT, dyT, a, w2, gate, offs, out):
             copy(result[:], dw[:])
             nc.sync.dma_start(out=out[e, b * P:(b + 1) * P, :], in_=result[:])
 
-        load_gate(0)
+        load_gate()
         load_dy(0)
         nc.sync.dma_start(offsets[:], offs)
-        load_gate(1)
         load_dy(1)
         load_x(0)
         load_dy(2)
@@ -222,6 +230,8 @@ def tile_moe_mlp_relu_kernel(tc, xT, dyT, a, w2, gate, offs, out):
         load_a(0)
         load_a(1)
 
+        spread_gate(0)
+        spread_gate(1)
         gather_dy(0, 0)
         gather_dy(1, 0)
         gather_dy(0, 1)
@@ -235,11 +245,15 @@ def tile_moe_mlp_relu_kernel(tc, xT, dyT, a, w2, gate, offs, out):
         gather_dy(1, 3)
         weave_g(0)
         weave_g(1)
-        weave_w(0)
-        quantize_w(0)
+        weave_w(0, 0, H // 2)
+        weave_w(0, H // 2, H)
+        quantize_w(0, 0, H // 2)
+        quantize_w(0, H // 2, H)
         quantize_g(0)
-        weave_w(1)
-        quantize_w(1)
+        weave_w(1, 0, H // 2)
+        weave_w(1, H // 2, H)
+        quantize_w(1, 0, H // 2)
+        quantize_w(1, H // 2, H)
         quantize_g(1)
         cast_x(1)
         gather_x(0, 1)

from contextlib import ExitStack

import concourse.mybir as mybir
from concourse.masks import make_identity

K, T, E, C, H, N = 256, 1536, 2, 512, 512, 512
FLOPS = 2 * E * C * H * (N + K)

F32 = mybir.dt.float32
BF16 = mybir.dt.bfloat16
U32 = mybir.dt.uint32
U16 = mybir.dt.uint16
U8 = mybir.dt.uint8
E4M3 = mybir.dt.float8_e4m3fn_x4
E5M2 = mybir.dt.float8_e5m2_x4
COPY = mybir.ActivationFunctionType.Copy
IS_GT = mybir.AluOpType.is_gt
MULT = mybir.AluOpType.mult
ADD = mybir.AluOpType.add

P = 128
PACK = 4
LIST_COLS = C // 16


def tile_moe_mlp_relu_kernel(tc, xT, dyT, a, w2, gate, offs, out):
    nc = tc.nc
    with ExitStack() as ctx:
        keep = ctx.enter_context(tc.tile_pool(name="keep", bufs=1))
        turns = ctx.enter_context(tc.psum_pool(name="turns", bufs=4))
        sums = ctx.enter_context(tc.psum_pool(name="sums", bufs=4))

        shared = {"x_cast0":"gate_cols"}
        tiles = {}

        def sb(name, shape, dtype):
            if name not in tiles:
                tiles[name] = keep.tile(shape, dtype, name=name, tag=shared.get(name, name), align_bytes=64)
            return tiles[name]

        offsets = keep.tile([P, E * LIST_COLS], U16, name="offsets")
        identity = sb("identity", [P, P], F32)
        make_identity(nc, identity[:])

        def dy(t):
            return sb("dy%d" % t, [P, T], F32)

        def gates(e):
            return sb("gates%d" % e, [P, C], F32)

        def x_raw(b):
            return sb("x_raw%d" % b, [P, T], F32)

        def w_raw(e):
            return sb("w_raw%d" % e, [P, PACK, H], F32)

        def a_raw(e, b):
            return sb("a_raw%d_%d" % (e, b), [P, C], F32)

        def g_rows(e):
            return sb("g_rows%d" % e, [P, PACK, C], F32)

        def g_in(e):
            return sb("g_in%d" % e, [P, C, PACK], BF16)

        def w_in(e):
            return sb("w_in%d" % e, [P, H, PACK], BF16)

        def x_cast(b):
            return sb("x_cast%d" % b, [P, T], BF16)

        def x_picked(e, b):
            return sb("x_picked%d_%d" % (e, b), [P, C], BF16)

        def x_in(e):
            return sb("x_in%d" % e, [P, K * PACK], BF16)

        def da_rows(e, b):
            return sb("da_rows%d_%d" % (e, b), [P, C], BF16)

        def da_in(e, h):
            return sb("da_in%d_%d" % (e, h), [P, H * PACK // 2], BF16)

        def codes(name, e, width):
            return sb("%s_codes%d" % (name, e), [P, width], U32)

        def scales(name, e, width):
            return sb("%s_scales%d" % (name, e), [P, width], U8)

        def load_dy(t):
            nc.sync.dma_start(out=dy(t)[:], in_=dyT.rearrange("(p t) c -> p t c", t=PACK)[:, t, :])

        def gate_cols():
            return sb("gate_cols", [P, E, PACK], F32)

        def load_gate():
            nc.sync.dma_start(out=gate_cols()[:], in_=gate[0, :].rearrange("(e q r) -> q e r", e=E, r=PACK))

        def spread_gate(e):
            bank = turns.tile([P, PACK, P], F32, name="bank", tag="bank")
            for r in range(PACK):
                nc.tensor.transpose(bank[:, r, :], gate_cols()[:, e, r:r + 1].to_broadcast([P, P]), identity[:])
            nc.scalar.copy(gates(e)[:].rearrange("p (q r) -> p q r", r=PACK), bank[:].rearrange("p r q -> p q r"))

        def load_x(b):
            nc.sync.dma_start(out=x_raw(b)[:], in_=xT[b * P:(b + 1) * P, :])

        def load_w(e):
            nc.sync.dma_start(out=w_raw(e)[:], in_=w2[e].rearrange("(p t) i -> p t i", t=PACK))

        def load_a(e):
            for b in range(H // P):
                nc.sync.dma_start(out=a_raw(e, b)[:], in_=a[b * P:(b + 1) * P, e * C:(e + 1) * C])

        def slots(e):
            return offsets[:, e * LIST_COLS:(e + 1) * LIST_COLS]

        def gather_dy(e, t):
            nc.vector.tensor_tensor(g_rows(e)[:, t, :], dy(t)[:].indirect(slots(e)), gates(e)[:], MULT)

        def weave(copy, woven, rows, first, last):
            copy(
                woven[:, first:last, :].rearrange("p (c i) t -> p c t i", i=4),
                rows[:, :, first:last].rearrange("p t (c i) -> p c t i", i=4),
            )

        def gate_weave(e, first, last):
            nc.vector.tensor_tensor(
                g_in(e)[:, first:last, :].rearrange("p (c i) t -> p c t i", i=4),
                g_rows(e)[:, :, first:last].rearrange("p t (c i) -> p c t i", i=4),
                gates(e)[:, first:last].rearrange("p (c i) -> p c i", i=4).unsqueeze(2).to_broadcast([P, (last - first) // 4, PACK, 4]),
                MULT,
            )

        def pool_copy(target, source):
            nc.gpsimd.tensor_scalar(target, source, 1.0, 0.0, MULT, ADD)

        def weave_g(e, first=0, last=C, copy=nc.scalar.copy):
            weave(copy, g_in(e), g_rows(e), first, last)

        def weave_w(e, first=0, last=H, copy=nc.vector.tensor_copy):
            weave(copy, w_in(e), w_raw(e), first, last)

        def quantize(name, e, width, values, fmt, cols):
            nc.vector.quantize_mx(out=codes(name, e, width)[:, cols].bitcast(fmt), scales=scales(name, e, width)[:, cols], in_=values)

        def quantize_g(e):
            quantize("g", e, C, g_in(e)[:].rearrange("p c t -> p (c t)"), E5M2, slice(0, C))

        def quantize_w(e, first=0, last=H):
            quantize("w", e, H, w_in(e)[:, first:last, :].rearrange("p c t -> p (c t)"), E4M3, slice(first, last))

        def quantize_x(e):
            quantize("x", e, K, x_in(e)[:], E4M3, slice(0, K))

        def quantize_da(e, h):
            quantize("da", e, H, da_in(e, h)[:], E5M2, slice(h * H // 2, (h + 1) * H // 2))

        def cast_x(b, copy=nc.scalar.copy):
            copy(x_cast(b)[:], x_raw(b)[:])

        def gather_x(e, b):
            nc.scalar.activation(x_picked(e, b)[:], x_cast(b)[:].indirect(slots(e)), COPY)

        def turn(pool, halves, target, copy):
            count = len(halves)
            bank = pool.tile([P, 2, 2, P], F32, name="bank", tag="bank")
            for s in range(count):
                for u in range(2):
                    nc.tensor.transpose(bank[:, s, u, :], halves[s][u], identity[:])
            copy(
                target.rearrange("p (s c u) -> p s c u", s=count, u=2),
                bank[:, 0:count, :, :].rearrange("p s u c -> p s c u"),
            )

        def turn_x(e, first=0, count=2, pool=turns, copy=nc.scalar.copy):
            words = [x_picked(e, first + b)[:].bitcast(F32) for b in range(count)]
            target = x_in(e)[:].bitcast(F32)[:, first * 2 * P:(first + count) * 2 * P]
            turn(pool, [[w[:, u::2] for u in range(2)] for w in words], target, copy)

        def turn_da(e, first, count, pool=turns, copy=nc.scalar.copy):
            words = [da_rows(e, first + s)[:].bitcast(F32) for s in range(count)]
            start = (first % 2) * 2 * P
            target = da_in(e, first // 2)[:].bitcast(F32)[:, start:start + count * 2 * P]
            turn(pool, [[w[:, u * P:(u + 1) * P] for u in range(2)] for w in words], target, copy)

        def product(left, right, e, b, width, bank):
            cols = slice(b * P, (b + 1) * P)
            nc.tensor.matmul_mx(
                out=bank[:],
                lhsT=codes(left, e, width)[:, cols].bitcast(E4M3), lhsT_scale=scales(left, e, width)[:, cols],
                rhs=codes(right, e, C)[:].bitcast(E5M2), rhs_scale=scales(right, e, C)[:],
                start=True, stop=True,
            )

        banks = {}

        def first_product(e, b):
            banks[e, b] = sums.tile([P, C], F32, name="dh", tag="bank")
            product("w", "g", e, b, H, banks[e, b])

        def mask(e, b):
            dh = banks[e, b]
            for u in range(2):
                nc.vector.scalar_tensor_tensor(
                    da_rows(e, b)[:].rearrange("i (u q r) -> i u q r", u=2, r=2)[:, u],
                    a_raw(e, b)[:].rearrange("i (q u r) -> i u q r", u=2, r=2)[:, u],
                    0.0,
                    dh[:].rearrange("i (q u r) -> i u q r", u=2, r=2)[:, u],
                    IS_GT, MULT,
                )

        def second_product(e, b, copy=nc.scalar.copy):
            dw = sums.tile([P, H], F32, name="dw", tag="bank")
            product("x", "da", e, b, K, dw)
            result = sb("result%d_%d" % (e, b), [P, H], F32)
            copy(result[:], dw[:])
            nc.sync.dma_start(out=out[e, b * P:(b + 1) * P, :], in_=result[:])

        load_gate()
        load_dy(0)
        nc.sync.dma_start(offsets[:], offs)
        load_dy(1)
        load_x(0)
        load_dy(2)
        load_dy(3)
        load_w(0)
        load_w(1)
        load_x(1)
        load_a(0)
        load_a(1)

        spread_gate(0)
        spread_gate(1)
        gather_dy(0, 0)
        gather_dy(1, 0)
        gather_dy(0, 1)
        gather_dy(1, 1)
        cast_x(0)
        gather_x(0, 0)
        gather_x(1, 0)
        gather_dy(0, 2)
        gather_dy(1, 2)
        gather_dy(0, 3)
        gather_dy(1, 3)
        weave_g(0)
        weave_g(1)
        weave_w(0, 0, H // 2)
        weave_w(0, H // 2, H)
        quantize_w(0, 0, H // 2)
        quantize_w(0, H // 2, H)
        quantize_g(0)
        weave_w(1, 0, H // 2)
        weave_w(1, H // 2, H)
        quantize_w(1, 0, H // 2)
        quantize_w(1, H // 2, H)
        quantize_g(1)
        cast_x(1)
        gather_x(0, 1)
        gather_x(1, 1)
        first_product(0, 0)
        first_product(0, 1)
        first_product(0, 2)
        first_product(0, 3)
        mask(0, 0)
        first_product(1, 0)
        mask(0, 1)
        first_product(1, 1)
        mask(0, 2)
        first_product(1, 2)
        mask(0, 3)
        first_product(1, 3)
        mask(1, 0)
        mask(1, 1)
        mask(1, 2)
        mask(1, 3)
        turn_da(0, 0, 2)
        turn_da(0, 2, 2)
        turn_x(0)
        turn_x(1)
        turn_da(1, 0, 2)
        turn_da(1, 2, 1)
        turn_da(1, 3, 1, copy=nc.vector.tensor_copy)
        quantize_da(0, 0)
        quantize_da(0, 1)
        quantize_x(0)
        quantize_da(1, 0)
        quantize_x(1)
        quantize_da(1, 1)
        second_product(0, 0)
        second_product(0, 1)
        second_product(1, 0)
        second_product(1, 1, nc.vector.tensor_copy)
